import numpy as np
import ml_dtypes


def mxq(x, axis, fmt="e4m3"):
    dtype, down = {"e4m3": (ml_dtypes.float8_e4m3fn, 7), "e5m2": (ml_dtypes.float8_e5m2, 14)}[fmt]
    v = np.moveaxis(np.asarray(x, np.float32).astype(ml_dtypes.bfloat16).astype(np.float64), axis, -1)
    blocks = v.reshape(v.shape[:-1] + (-1, 32))
    amax = np.abs(blocks).max(-1, keepdims=True)
    byte = np.maximum(np.where(amax > 0, np.frexp(amax)[1] - 1 + 127, 0) - down, 1)
    scale = np.exp2(byte - 127.0)
    codes = (blocks / scale).astype(np.float32).astype(dtype).astype(np.float64)
    return np.moveaxis((codes * scale).reshape(v.shape), -1, axis)


WIDE = False


def mx_kscale(k, group=512):
    if not WIDE:
        return np.ones(k)
    levels = np.array([18, -18])
    if group != 512:
        return np.exp2(np.random.permutation(np.resize(levels, k // group))).repeat(group)
    if k % 512:
        return np.exp2(np.random.permutation(np.resize(levels, k // 32))).repeat(32)
    a = np.empty((k // 512, 16))
    for p in range(k // 512):
        a[p, :8] = np.random.permutation(np.resize(levels, 8))
        for g in range(8):
            far = levels[np.abs(levels - a[p, g]) >= 10]
            a[p, g + 8] = far[np.random.randint(len(far))]
    return np.exp2(a.ravel()).repeat(32)


def f64(x):
    return np.asarray(x).astype(np.float64)


def silu(v):
    return v / (1.0 + np.exp(-v))


G, D, I, Q, E = 8, 128, 128, 128, 128


def sgn(shape):
    return np.random.uniform(0.5, 2.0, shape) * np.where(np.random.standard_normal(shape) < 0, -1.0, 1.0)


def setup_inputs():
    n = np.random.standard_normal
    s_d = mx_kscale(D, 0)
    s_i = mx_kscale(I, 0)
    return {
        "kT": (n((G, D, I)) / np.sqrt(D) / s_d[:, None]).astype(np.float32),
        "qT": (n((G, D, Q)) * s_d[:, None]).astype(np.float32),
        "dk": (np.exp(-np.random.uniform(0.0, 3.0, (G, I, Q))) * (np.arange(I)[:, None] <= np.arange(Q)[None])).astype(np.float32),
        "t": (sgn((G, I, 1)) * s_i[:, None]).astype(np.float32),
        "v": ((n((G, I, E))) / s_i[:, None]).astype(np.float32),
        "xs": (n((G, Q, E))).astype(np.float32),
        "ds": (np.random.uniform(0.5, 2.0, (G, Q, 1))).astype(np.float32),
        "zg": (n((G, Q, E))).astype(np.float32),
    }


def reference(kT, qT, dk, t, v, xs, ds, zg):
    kTq = mxq(f64(kT), 1, "e4m3")
    qTq = mxq(f64(qT), 1, "e4m3")
    z = kTq.transpose(0, 2, 1) @ qTq
    p = z * f64(dk) * f64(t)
    pq = mxq(p, 1, "e4m3")
    vq = mxq(f64(v), 1, "e4m3")
    y = pq.transpose(0, 2, 1) @ vq
    o = (y + f64(ds) * f64(xs)) * silu(f64(zg))
    return o

@@ -1,0 +1,255 @@
+from contextlib import ExitStack
+
+import concourse.mybir as mybir
+
+F32 = mybir.dt.float32
+BF16 = mybir.dt.bfloat16
+U32 = mybir.dt.uint32
+U8 = mybir.dt.uint8
+FP8X4 = mybir.dt.float8_e4m3fn_x4
+ACT = mybir.ActivationFunctionType
+ALU = mybir.AluOpType
+
+P = 128
+W = 128
+R = 32
+PACK = 4
+SETS = 2
+TILES = 4
+FLOPS = 2 * 2 * 8 * 128 * 128 * 128
+
+
+def tile_rows_win_ssd_skip_kernel(tc, kT, qT, dk, t, v, xs, ds, zg, out):
+    nc = tc.nc
+    with ExitStack() as ctx:
+        sb = ctx.enter_context(tc.tile_pool(name="sb", bufs=1))
+        ps = ctx.enter_context(tc.psum_pool(name="ps", bufs=1))
+        ctx.enter_context(tc.manual_schedule())
+
+        def per_set(name, shape, dtype):
+            return [sb.tile(shape, dtype, name=name + str(x), align_bytes=64) for x in range(SETS)]
+
+        k_raw = per_set("k_raw", [P, PACK, W], F32)
+        q_raw = per_set("q_raw", [P, PACK, W], F32)
+        v_raw = per_set("v_raw", [P, PACK, W], F32)
+        dk_raw = per_set("dk_raw", [P, PACK, W], F32)
+        dkt = per_set("dkt", [P, PACK, W], F32)
+        z_sb = per_set("z_sb", [P, W, PACK], F32)
+        k_bf = per_set("k_bf", [P, W, PACK], BF16)
+        q_bf = per_set("q_bf", [P, W, PACK], BF16)
+        v_bf = per_set("v_bf", [P, W, PACK], BF16)
+        p_bf = per_set("p_bf", [P, W, PACK], BF16)
+        xs_sb = per_set("xs_sb", [P, TILES, W], F32)
+        zg_sb = per_set("zg_sb", [P, TILES, W], F32)
+        gate = per_set("gate", [P, TILES, W], F32)
+        summed = per_set("summed", [P, TILES, W], F32)
+        result = per_set("result", [P, TILES, W], F32)
+        p_codes = per_set("p_codes", [P, W], U32)
+        p_scales = per_set("p_scales", [P, W], U8)
+        v_codes = per_set("v_codes", [P, W], U32)
+        v_scales = per_set("v_scales", [P, W], U8)
+        kq_codes = sb.tile([P, 5 * W], U32, align_bytes=64)
+        kq_scales = sb.tile([P, 5 * W], U8, align_bytes=64)
+        k_scales_shifted = sb.tile([P, 5 * W], U8, align_bytes=64)
+        t_sb = sb.tile([P, SETS, 8], F32, align_bytes=64)
+        ds_rows = sb.tile([P, R], F32, align_bytes=64)
+        ds_cols = sb.tile([P, R], F32, align_bytes=64)
+        warm = sb.tile([P, 8], F32, align_bytes=64)
+        banks = [[ps.tile([P, PACK, W], F32, name="bank%d%d" % (x, r)) for r in range(TILES)] for x in range(SETS)]
+
+        def windows(x):
+            return slice(TILES * x, TILES * (x + 1))
+
+        def rows(r):
+            return slice(R * r, R * (r + 1))
+
+        def load_packed(dst, src, x):
+            nc.sync.dma_start(out=dst[x][:], in_=src[windows(x)].rearrange("g (s j) c -> (g s) j c", j=PACK))
+
+        def load_rows(dst, src, x, lo, hi):
+            nc.sync.dma_start(
+                out=dst[x][:, lo:hi, :], in_=src[TILES * x + lo : TILES * x + hi].rearrange("g q e -> q g e")
+            )
+
+        def store(x, lo, hi):
+            nc.sync.dma_start(
+                out=out[TILES * x + lo : TILES * x + hi].rearrange("g q e -> q g e"), in_=result[x][:, lo:hi, :]
+            )
+
+        def k_col(x):
+            return W + 2 * W * x
+
+        def q_col(x):
+            return 2 * W + 2 * W * x
+
+        def deal_k(x):
+            nc.scalar.copy(
+                out=k_bf[x][:].rearrange("p (j s) u -> p j s u", j=PACK),
+                in_=k_raw[x][:].rearrange("p u (s j) -> p j s u", j=PACK),
+            )
+
+        def interleave(engine, dst, src):
+            engine.tensor_copy(out=dst[:], in_=src[:].rearrange("p u c -> p c u"))
+
+        def quantize(codes, scales, src):
+            nc.vector.quantize_mx(out=codes.bitcast(FP8X4), scales=scales, in_=src[:].rearrange("p c u -> p (c u)"))
+
+        def quantize_kq(x):
+            kc, qc = k_col(x), q_col(x)
+            quantize(kq_codes[:, kc : kc + W], kq_scales[:, kc : kc + W], k_bf[x])
+            quantize(kq_codes[:, qc : qc + W], kq_scales[:, qc : qc + W], q_bf[x])
+            nc.vector.tensor_copy(out=k_scales_shifted[:, kc - R : kc - R + W], in_=kq_scales[:, kc : kc + W])
+
+        def scores(x):
+            qc = q_col(x)
+            for step in range(PACK):
+                for r in range(TILES):
+                    j = (r + (0, 2, 1, 3)[step]) % PACK
+                    c = k_col(x) + R * (j - r)
+                    if (j - r) % 2 == 0:
+                        plane = kq_scales[rows(r), c : c + W]
+                    else:
+                        plane = k_scales_shifted[rows(r), c - R : c - R + W]
+                    nc.tensor.matmul_mx(
+                        out=banks[x][r][:, j, :],
+                        lhsT=kq_codes[rows(r), c : c + W].bitcast(FP8X4),
+                        lhsT_scale=plane,
+                        rhs=kq_codes[rows(r), qc : qc + W].bitcast(FP8X4),
+                        rhs_scale=kq_scales[rows(r), qc : qc + W],
+                        start=True,
+                        stop=True,
+                    )
+
+        def decay_times_t(x):
+            for j in range(PACK):
+                nc.scalar.activation(
+                    out=dkt[x][:, j, :], in_=dk_raw[x][:, j, :], func=ACT.Copy, scale=t_sb[:, x, j : j + 1]
+                )
+
+        def weigh_from_psum(x, r):
+            nc.vector.tensor_tensor(
+                out=p_bf[x][rows(r)],
+                in0=banks[x][r][rows(r)].rearrange("p j q -> p q j"),
+                in1=dkt[x][rows(r)].rearrange("p j q -> p q j"),
+                op=ALU.mult,
+            )
+
+        def evacuate(x, r):
+            nc.scalar.copy(out=z_sb[x][rows(r)], in_=banks[x][r][rows(r)].rearrange("p j q -> p q j"))
+
+        def weigh_from_sbuf(x, n):
+            nc.vector.tensor_tensor(
+                out=p_bf[x][0 : R * n],
+                in0=z_sb[x][0 : R * n],
+                in1=dkt[x][0 : R * n].rearrange("p j q -> p q j"),
+                op=ALU.mult,
+            )
+
+        def interleave_v(x):
+            nc.gpsimd.tensor_scalar(
+                out=v_bf[x][:],
+                in0=v_raw[x][:].rearrange("p u c -> p c u"),
+                scalar1=1.0,
+                scalar2=0.0,
+                op0=ALU.mult,
+                op1=ALU.add,
+            )
+
+        def values(x):
+            for r in range(TILES):
+                nc.tensor.matmul_mx(
+                    out=banks[x][r][:, 0, :],
+                    lhsT=p_codes[x][rows(r), :].bitcast(FP8X4),
+                    lhsT_scale=p_scales[x][rows(r), :],
+                    rhs=v_codes[x][rows(r), :].bitcast(FP8X4),
+                    rhs_scale=v_scales[x][rows(r), :],
+                    start=True,
+                    stop=True,
+                )
+
+        def add_skip(x, r):
+            g = TILES * x + r
+            nc.vector.scalar_tensor_tensor(
+                out=summed[x][:, r, :],
+                in0=xs_sb[x][:, r, :],
+                scalar=ds_cols[:, g : g + 1],
+                in1=banks[x][r][:, 0, :],
+                op0=ALU.mult,
+                op1=ALU.add,
+            )
+
+        def silu(x, lo, hi):
+            nc.scalar.activation(out=gate[x][:, lo:hi, :], in_=zg_sb[x][:, lo:hi, :], func=ACT.Silu)
+
+        def apply_gate(engine, x, lo, hi):
+            engine.tensor_tensor(
+                out=result[x][:, lo:hi, :], in0=summed[x][:, lo:hi, :], in1=gate[x][:, lo:hi, :], op=ALU.mult
+            )
+
+        nc.vector.memset(warm[:], 0.0)
+        nc.vector.memset(ds_rows[:], 0.0)
+        nc.vector.memset(kq_codes[:, 0:W], 0)
+        nc.vector.memset(kq_scales[:].bitcast(U32), 0)
+        nc.vector.memset(k_scales_shifted[:].bitcast(U32), 0)
+        nc.scalar.activation(out=warm[:, 4:5], in_=warm[:, 0:1], func=ACT.Silu)
+
+        load_packed(k_raw, kT, 0)
+        load_packed(q_raw, qT, 0)
+        nc.sync.dma_start(out=t_sb[:, :, 0:PACK], in_=t.rearrange("(x g) (s j) o -> (g s) x (j o)", x=SETS, j=PACK))
+        load_packed(dk_raw, dk, 0)
+        load_packed(k_raw, kT, 1)
+        load_packed(q_raw, qT, 1)
+        load_packed(dk_raw, dk, 1)
+        load_packed(v_raw, v, 0)
+        for a in range(TILES):
+            nc.sync.dma_start(out=ds_rows[R * a : R * a + 8, :], in_=ds[:, rows(a), :].rearrange("g q o -> g (q o)"))
+        load_packed(v_raw, v, 1)
+        load_rows(xs_sb, xs, 0, 0, 4)
+        load_rows(zg_sb, zg, 0, 0, 4)
+        load_rows(xs_sb, xs, 1, 0, 4)
+        load_rows(zg_sb, zg, 1, 0, 2)
+        load_rows(zg_sb, zg, 1, 2, 4)
+
+        deal_k(0)
+        interleave(nc.vector, q_bf[0], q_raw[0])
+        quantize_kq(0)
+        scores(0)
+        decay_times_t(0)
+        deal_k(1)
+        weigh_from_psum(0, 3)
+        interleave(nc.vector, q_bf[1], q_raw[1])
+        quantize_kq(1)
+        scores(1)
+        evacuate(0, 0)
+        evacuate(0, 1)
+        weigh_from_psum(0, 2)
+        interleave_v(0)
+        decay_times_t(1)
+        weigh_from_sbuf(0, 2)
+        quantize(v_codes[0][:], v_scales[0][:], v_bf[0])
+        quantize(p_codes[0][:], p_scales[0][:], p_bf[0])
+        values(0)
+        for r in range(3):
+            evacuate(1, r)
+        weigh_from_psum(1, 3)
+        interleave_v(1)
+        nc.vector.transpose(out=ds_cols[:], in_=ds_rows[:])
+        weigh_from_sbuf(1, 3)
+        quantize(v_codes[1][:], v_scales[1][:], v_bf[1])
+        quantize(p_codes[1][:], p_scales[1][:], p_bf[1])
+        values(1)
+        silu(0, 0, 4)
+        for r in range(TILES):
+            add_skip(0, r)
+        apply_gate(nc.gpsimd, 0, 0, 2)
+        silu(1, 0, 2)
+        silu(1, 2, 4)
+        for r in range(TILES):
+            add_skip(1, r)
+        store(0, 0, 2)
+        apply_gate(nc.vector, 0, 2, 4)
+        store(0, 2, 4)
+        apply_gate(nc.vector, 1, 0, 2)
+        store(1, 0, 2)
+        apply_gate(nc.vector, 1, 2, 4)
+        store(1, 2, 4)

@@ -14,9 +14,15 @@ P = 128
 W = 128
 R = 32
 PACK = 4
-SETS = 2
 TILES = 4
-FLOPS = 2 * 2 * 8 * 128 * 128 * 128
+SETS = 2
+WINDOWS = SETS * TILES
+FLOPS = 2 * 2 * WINDOWS * W * W * W
+
+K_COL = W
+Q_COL = 2 * W
+SHIFTS = (0, 2, 1, 3)
+COPIED = 3
 
 
 def tile_rows_win_ssd_skip_kernel(tc, kT, qT, dk, t, v, xs, ds, zg, out):
@@ -26,230 +32,215 @@ def tile_rows_win_ssd_skip_kernel(tc, kT, qT, dk, t, v, xs, ds, zg, out):
         ps = ctx.enter_context(tc.psum_pool(name="ps", bufs=1))
         ctx.enter_context(tc.manual_schedule())
 
+        def tile(name, shape, dtype):
+            return sb.tile(shape, dtype, name=name, align_bytes=64)
+
         def per_set(name, shape, dtype):
-            return [sb.tile(shape, dtype, name=name + str(x), align_bytes=64) for x in range(SETS)]
+            return [tile(name + str(x), shape, dtype) for x in range(SETS)]
 
         k_raw = per_set("k_raw", [P, PACK, W], F32)
         q_raw = per_set("q_raw", [P, PACK, W], F32)
-        v_raw = per_set("v_raw", [P, PACK, W], F32)
-        dk_raw = per_set("dk_raw", [P, PACK, W], F32)
-        dkt = per_set("dkt", [P, PACK, W], F32)
-        z_sb = per_set("z_sb", [P, W, PACK], F32)
+        v_raw = tile("v_raw", [P, SETS, PACK, W], F32)
+        p_packed = per_set("p_packed", [P, PACK, W], BF16)
         k_bf = per_set("k_bf", [P, W, PACK], BF16)
         q_bf = per_set("q_bf", [P, W, PACK], BF16)
         v_bf = per_set("v_bf", [P, W, PACK], BF16)
         p_bf = per_set("p_bf", [P, W, PACK], BF16)
-        xs_sb = per_set("xs_sb", [P, TILES, W], F32)
-        zg_sb = per_set("zg_sb", [P, TILES, W], F32)
-        gate = per_set("gate", [P, TILES, W], F32)
-        summed = per_set("summed", [P, TILES, W], F32)
-        result = per_set("result", [P, TILES, W], F32)
         p_codes = per_set("p_codes", [P, W], U32)
         p_scales = per_set("p_scales", [P, W], U8)
         v_codes = per_set("v_codes", [P, W], U32)
         v_scales = per_set("v_scales", [P, W], U8)
-        kq_codes = sb.tile([P, 5 * W], U32, align_bytes=64)
-        kq_scales = sb.tile([P, 5 * W], U8, align_bytes=64)
-        k_scales_shifted = sb.tile([P, 5 * W], U8, align_bytes=64)
-        t_sb = sb.tile([P, SETS, 8], F32, align_bytes=64)
-        ds_rows = sb.tile([P, R], F32, align_bytes=64)
-        ds_cols = sb.tile([P, R], F32, align_bytes=64)
-        warm = sb.tile([P, 8], F32, align_bytes=64)
-        banks = [[ps.tile([P, PACK, W], F32, name="bank%d%d" % (x, r)) for r in range(TILES)] for x in range(SETS)]
-
-        def windows(x):
-            return slice(TILES * x, TILES * (x + 1))
+        kq_codes = tile("kq_codes", [P, 3 * W], U32)
+        kq_scales = tile("kq_scales", [P, 3 * W], U8)
+        k_scales_shifted = tile("k_scales_shifted", [P, 3 * W], U8)
+        dk_packed = tile("dk_packed", [P, PACK, W], F32)
+        t_packed = tile("t_packed", [P, 8], F32)
+        dk_t = tile("dk_t", [P, PACK, W], F32)
+        z_copied = tile("z_copied", [P, PACK, W], F32)
+        k_codes = tile("k_codes", [P, W], U32)
+        k_scales = tile("k_scales", [P, W], U8)
+        q_codes = tile("q_codes", [P, W], U32)
+        q_scales = tile("q_scales", [P, W], U8)
+        dk_rows = tile("dk_rows", [P, TILES, W], F32)
+        p_rows = tile("p_rows", [P, TILES, W], BF16)
+        xs_sb = tile("xs_sb", [P, WINDOWS, W], F32)
+        zg_sb = tile("zg_sb", [P, WINDOWS, W], F32)
+        skip = tile("skip", [P, WINDOWS, W], F32)
+        gate = tile("gate", [P, WINDOWS, W], F32)
+        summed = tile("summed", [P, WINDOWS, W], F32)
+        result = tile("result", [P, WINDOWS, W], F32)
+        t_blocks = tile("t_blocks", [P, R], F32)
+        t_cols = tile("t_cols", [P, R], F32)
+        ds_blocks = tile("ds_blocks", [P, R], F32)
+        ds_cols = tile("ds_cols", [P, R], F32)
+        wide_banks = [ps.tile([P, PACK, W], F32, name="wide%d" % r) for r in range(TILES)]
+        narrow_banks = [ps.tile([P, W], F32, name="narrow%d" % r) for r in range(TILES)]
+        y_psum = [bank[:, 0, :] for bank in wide_banks] + [bank[:] for bank in narrow_banks]
 
         def rows(r):
             return slice(R * r, R * (r + 1))
 
         def load_packed(dst, src, x):
-            nc.sync.dma_start(out=dst[x][:], in_=src[windows(x)].rearrange("g (s j) c -> (g s) j c", j=PACK))
+            windows = src[TILES * x : TILES * (x + 1)]
+            nc.sync.dma_start(out=dst[:], in_=windows.rearrange("g (s j) c -> (g s) j c", j=PACK))
 
-        def load_rows(dst, src, x, lo, hi):
-            nc.sync.dma_start(
-                out=dst[x][:, lo:hi, :], in_=src[TILES * x + lo : TILES * x + hi].rearrange("g q e -> q g e")
-            )
+        def load_rows(dst, windows):
+            nc.sync.dma_start(out=dst, in_=windows.rearrange("g a b -> a g b"))
 
-        def store(x, lo, hi):
-            nc.sync.dma_start(
-                out=out[TILES * x + lo : TILES * x + hi].rearrange("g q e -> q g e"), in_=result[x][:, lo:hi, :]
-            )
-
-        def k_col(x):
-            return W + 2 * W * x
-
-        def q_col(x):
-            return 2 * W + 2 * W * x
-
-        def deal_k(x):
-            nc.scalar.copy(
-                out=k_bf[x][:].rearrange("p (j s) u -> p j s u", j=PACK),
-                in_=k_raw[x][:].rearrange("p u (s j) -> p j s u", j=PACK),
-            )
-
-        def interleave(engine, dst, src):
-            engine.tensor_copy(out=dst[:], in_=src[:].rearrange("p u c -> p c u"))
-
-        def quantize(codes, scales, src):
-            nc.vector.quantize_mx(out=codes.bitcast(FP8X4), scales=scales, in_=src[:].rearrange("p c u -> p (c u)"))
-
-        def quantize_kq(x):
-            kc, qc = k_col(x), q_col(x)
-            quantize(kq_codes[:, kc : kc + W], kq_scales[:, kc : kc + W], k_bf[x])
-            quantize(kq_codes[:, qc : qc + W], kq_scales[:, qc : qc + W], q_bf[x])
-            nc.vector.tensor_copy(out=k_scales_shifted[:, kc - R : kc - R + W], in_=kq_scales[:, kc : kc + W])
-
-        def scores(x):
-            qc = q_col(x)
-            for step in range(PACK):
-                for r in range(TILES):
-                    j = (r + (0, 2, 1, 3)[step]) % PACK
-                    c = k_col(x) + R * (j - r)
-                    if (j - r) % 2 == 0:
-                        plane = kq_scales[rows(r), c : c + W]
-                    else:
-                        plane = k_scales_shifted[rows(r), c - R : c - R + W]
-                    nc.tensor.matmul_mx(
-                        out=banks[x][r][:, j, :],
-                        lhsT=kq_codes[rows(r), c : c + W].bitcast(FP8X4),
-                        lhsT_scale=plane,
-                        rhs=kq_codes[rows(r), qc : qc + W].bitcast(FP8X4),
-                        rhs_scale=kq_scales[rows(r), qc : qc + W],
-                        start=True,
-                        stop=True,
-                    )
-
-        def decay_times_t(x):
-            for j in range(PACK):
-                nc.scalar.activation(
-                    out=dkt[x][:, j, :], in_=dk_raw[x][:, j, :], func=ACT.Copy, scale=t_sb[:, x, j : j + 1]
+        def load_blocks(queue, dst, windows):
+            count = windows.shape[0]
+            for a in range(TILES):
+                queue.dma_start(
+                    out=dst[R * a : R * a + count, :], in_=windows[:, rows(a), :].rearrange("g c o -> g (c o)")
                 )
 
-        def weigh_from_psum(x, r):
-            nc.vector.tensor_tensor(
-                out=p_bf[x][rows(r)],
-                in0=banks[x][r][rows(r)].rearrange("p j q -> p q j"),
-                in1=dkt[x][rows(r)].rearrange("p j q -> p q j"),
-                op=ALU.mult,
+        def interleave(copy, dst, src):
+            copy(out=dst[:], in_=src.rearrange("p j c -> p c j"))
+
+        def quantize(codes, scales, src):
+            nc.vector.quantize_mx(out=codes.bitcast(FP8X4), scales=scales, in_=src[:].rearrange("p c j -> p (c j)"))
+
+        def product(dst, r, lhs_codes, lhs_scales, rhs_codes, rhs_scales):
+            nc.tensor.matmul_mx(
+                out=dst,
+                lhsT=lhs_codes[rows(r)].bitcast(FP8X4),
+                lhsT_scale=lhs_scales[rows(r)],
+                rhs=rhs_codes[rows(r)].bitcast(FP8X4),
+                rhs_scale=rhs_scales[rows(r)],
+                start=True,
+                stop=True,
             )
 
-        def evacuate(x, r):
-            nc.scalar.copy(out=z_sb[x][rows(r)], in_=banks[x][r][rows(r)].rearrange("p j q -> p q j"))
-
-        def weigh_from_sbuf(x, n):
-            nc.vector.tensor_tensor(
-                out=p_bf[x][0 : R * n],
-                in0=z_sb[x][0 : R * n],
-                in1=dkt[x][0 : R * n].rearrange("p j q -> p q j"),
-                op=ALU.mult,
-            )
-
-        def interleave_v(x):
-            nc.gpsimd.tensor_scalar(
-                out=v_bf[x][:],
-                in0=v_raw[x][:].rearrange("p u c -> p c u"),
-                scalar1=1.0,
-                scalar2=0.0,
-                op0=ALU.mult,
-                op1=ALU.add,
+        def shifted_scores(r, shift):
+            j = (r + shift) % PACK
+            first = K_COL + R * (j - r)
+            if shift % 2 == 0:
+                scales = kq_scales[:, first : first + W]
+            else:
+                scales = k_scales_shifted[:, first - R : first - R + W]
+            queries = slice(Q_COL, Q_COL + W)
+            product(
+                wide_banks[r][:, j, :],
+                r,
+                kq_codes[:, first : first + W],
+                scales,
+                kq_codes[:, queries],
+                kq_scales[:, queries],
             )
 
         def values(x):
+            quantize(p_codes[x][:], p_scales[x][:], p_bf[x])
             for r in range(TILES):
-                nc.tensor.matmul_mx(
-                    out=banks[x][r][:, 0, :],
-                    lhsT=p_codes[x][rows(r), :].bitcast(FP8X4),
-                    lhsT_scale=p_scales[x][rows(r), :],
-                    rhs=v_codes[x][rows(r), :].bitcast(FP8X4),
-                    rhs_scale=v_scales[x][rows(r), :],
-                    start=True,
-                    stop=True,
-                )
+                product(y_psum[TILES * x + r], r, p_codes[x], p_scales[x], v_codes[x], v_scales[x])
 
-        def add_skip(x, r):
-            g = TILES * x + r
-            nc.vector.scalar_tensor_tensor(
-                out=summed[x][:, r, :],
-                in0=xs_sb[x][:, r, :],
-                scalar=ds_cols[:, g : g + 1],
-                in1=banks[x][r][:, 0, :],
-                op0=ALU.mult,
-                op1=ALU.add,
+        def scale_skip(g):
+            nc.scalar.activation(out=skip[:, g, :], in_=xs_sb[:, g, :], func=ACT.Copy, scale=ds_cols[:, g : g + 1])
+
+        def add_skip(g):
+            nc.vector.tensor_tensor(out=summed[:, g, :], in0=y_psum[g], in1=skip[:, g, :], op=ALU.add)
+
+        def silu(lo, hi):
+            nc.scalar.activation(out=gate[:, lo:hi, :], in_=zg_sb[:, lo:hi, :], func=ACT.Silu)
+
+        def apply_gate(lo, hi):
+            nc.vector.tensor_tensor(
+                out=result[:, lo:hi, :], in0=summed[:, lo:hi, :], in1=gate[:, lo:hi, :], op=ALU.mult
             )
 
-        def silu(x, lo, hi):
-            nc.scalar.activation(out=gate[x][:, lo:hi, :], in_=zg_sb[x][:, lo:hi, :], func=ACT.Silu)
+        def store(lo, hi):
+            nc.sync.dma_start(out=out[lo:hi].rearrange("g q e -> q g e"), in_=result[:, lo:hi, :])
 
-        def apply_gate(engine, x, lo, hi):
-            engine.tensor_tensor(
-                out=result[x][:, lo:hi, :], in0=summed[x][:, lo:hi, :], in1=gate[x][:, lo:hi, :], op=ALU.mult
-            )
+        nc.scalar.dma_start(out=t_packed[:, 0:PACK], in_=t[0:TILES].rearrange("g (s j) o -> (g s) (j o)", j=PACK))
 
-        nc.vector.memset(warm[:], 0.0)
-        nc.vector.memset(ds_rows[:], 0.0)
-        nc.vector.memset(kq_codes[:, 0:W], 0)
+        nc.vector.memset(ds_cols[:], 0.0)
+        nc.vector.memset(kq_codes[:, 0:K_COL], 0)
         nc.vector.memset(kq_scales[:].bitcast(U32), 0)
         nc.vector.memset(k_scales_shifted[:].bitcast(U32), 0)
-        nc.scalar.activation(out=warm[:, 4:5], in_=warm[:, 0:1], func=ACT.Silu)
+        nc.gpsimd.memset(ds_blocks[:], 0.0)
+        nc.scalar.activation(out=t_blocks[:], in_=ds_cols[:], func=ACT.Silu)
 
-        load_packed(k_raw, kT, 0)
-        load_packed(q_raw, qT, 0)
-        nc.sync.dma_start(out=t_sb[:, :, 0:PACK], in_=t.rearrange("(x g) (s j) o -> (g s) x (j o)", x=SETS, j=PACK))
-        load_packed(dk_raw, dk, 0)
-        load_packed(k_raw, kT, 1)
-        load_packed(q_raw, qT, 1)
-        load_packed(dk_raw, dk, 1)
-        load_packed(v_raw, v, 0)
-        for a in range(TILES):
-            nc.sync.dma_start(out=ds_rows[R * a : R * a + 8, :], in_=ds[:, rows(a), :].rearrange("g q o -> g (q o)"))
-        load_packed(v_raw, v, 1)
-        load_rows(xs_sb, xs, 0, 0, 4)
-        load_rows(zg_sb, zg, 0, 0, 4)
-        load_rows(xs_sb, xs, 1, 0, 4)
-        load_rows(zg_sb, zg, 1, 0, 2)
-        load_rows(zg_sb, zg, 1, 2, 4)
+        for x in range(SETS):
+            load_packed(k_raw[x], kT, x)
+            load_packed(q_raw[x], qT, x)
+        load_blocks(nc.sync, t_blocks, t[TILES:WINDOWS])
+        load_blocks(nc.gpsimd, ds_blocks, ds)
+        load_packed(dk_packed, dk, 0)
+        load_rows(dk_rows[:], dk[TILES:WINDOWS])
+        nc.sync.dma_start(out=v_raw[:], in_=v.rearrange("(x g) (s j) c -> (g s) x j c", x=SETS, j=PACK))
+        load_rows(xs_sb[:, 0:TILES, :], xs[0:TILES])
+        load_rows(zg_sb[:, 0:TILES, :], zg[0:TILES])
 
-        deal_k(0)
-        interleave(nc.vector, q_bf[0], q_raw[0])
-        quantize_kq(0)
-        scores(0)
-        decay_times_t(0)
-        deal_k(1)
-        weigh_from_psum(0, 3)
-        interleave(nc.vector, q_bf[1], q_raw[1])
-        quantize_kq(1)
-        scores(1)
-        evacuate(0, 0)
-        evacuate(0, 1)
-        weigh_from_psum(0, 2)
-        interleave_v(0)
-        decay_times_t(1)
-        weigh_from_sbuf(0, 2)
+        nc.vector.tensor_copy(
+            out=k_bf[0][:].rearrange("p (j s) u -> p j s u", j=PACK),
+            in_=k_raw[0][:].rearrange("p u (s j) -> p j s u", j=PACK),
+        )
+        interleave(nc.vector.tensor_copy, q_bf[0], q_raw[0][:])
+        quantize(kq_codes[:, K_COL : K_COL + W], kq_scales[:, K_COL : K_COL + W], k_bf[0])
+        quantize(kq_codes[:, Q_COL : Q_COL + W], kq_scales[:, Q_COL : Q_COL + W], q_bf[0])
+        nc.vector.tensor_copy(out=k_scales_shifted[:, K_COL - R : K_COL - R + W], in_=kq_scales[:, K_COL : K_COL + W])
+        for shift in SHIFTS:
+            shifted_scores(0, shift)
+            shifted_scores(1, shift)
+
+        interleave(nc.scalar.copy, k_bf[1], k_raw[1][:])
+        interleave(nc.vector.tensor_copy, q_bf[1], q_raw[1][:])
+        quantize(k_codes[:], k_scales[:], k_bf[1])
+        quantize(q_codes[:], q_scales[:], q_bf[1])
+        nc.vector.transpose(out=t_cols[:], in_=t_blocks[:])
+        for r, shift in enumerate(SHIFTS):
+            shifted_scores(2, shift)
+            product(narrow_banks[r][:], r, k_codes, k_scales, q_codes, q_scales)
+        for shift in SHIFTS:
+            shifted_scores(3, shift)
+
+        for j in range(PACK):
+            nc.vector.tensor_scalar(
+                out=dk_t[:, j, :], in0=dk_packed[:, j, :], scalar1=t_packed[:, j : j + 1], scalar2=None, op0=ALU.mult
+            )
+        for r in range(TILES):
+            nc.vector.scalar_tensor_tensor(
+                out=p_rows[:, r, :],
+                in0=narrow_banks[r][:],
+                scalar=t_cols[:, r : r + 1],
+                in1=dk_rows[:, r, :],
+                op0=ALU.mult,
+                op1=ALU.mult,
+            )
+            nc.sync.dma_start(out=p_packed[1][rows(r)], in_=p_rows[:, r, :])
+        load_rows(xs_sb[:, TILES:WINDOWS, :], xs[TILES:WINDOWS])
+        load_rows(zg_sb[:, TILES:WINDOWS, :], zg[TILES:WINDOWS])
+
+        for r in range(COPIED):
+            nc.scalar.copy(out=z_copied[rows(r)], in_=wide_banks[r][rows(r)])
+        last = rows(COPIED)
+        nc.vector.tensor_tensor(out=p_packed[0][last], in0=wide_banks[COPIED][last], in1=dk_t[last], op=ALU.mult)
+        copied = slice(0, R * COPIED)
+        nc.vector.tensor_tensor(out=p_packed[0][copied], in0=z_copied[copied], in1=dk_t[copied], op=ALU.mult)
+
+        nc.vector.transpose(out=ds_cols[:], in_=ds_blocks[:])
+        for x in range(SETS):
+            interleave(nc.scalar.copy, v_bf[x], v_raw[:, x])
+        interleave(nc.vector.tensor_copy, p_bf[0], p_packed[0][:])
         quantize(v_codes[0][:], v_scales[0][:], v_bf[0])
-        quantize(p_codes[0][:], p_scales[0][:], p_bf[0])
         values(0)
-        for r in range(3):
-            evacuate(1, r)
-        weigh_from_psum(1, 3)
-        interleave_v(1)
-        nc.vector.transpose(out=ds_cols[:], in_=ds_rows[:])
-        weigh_from_sbuf(1, 3)
         quantize(v_codes[1][:], v_scales[1][:], v_bf[1])
-        quantize(p_codes[1][:], p_scales[1][:], p_bf[1])
+        for g in range(TILES):
+            scale_skip(g)
+        interleave(nc.vector.tensor_copy, p_bf[1], p_packed[1][:])
+        add_skip(0)
         values(1)
-        silu(0, 0, 4)
-        for r in range(TILES):
-            add_skip(0, r)
-        apply_gate(nc.gpsimd, 0, 0, 2)
-        silu(1, 0, 2)
-        silu(1, 2, 4)
-        for r in range(TILES):
-            add_skip(1, r)
-        store(0, 0, 2)
-        apply_gate(nc.vector, 0, 2, 4)
-        store(0, 2, 4)
-        apply_gate(nc.vector, 1, 0, 2)
-        store(1, 0, 2)
-        apply_gate(nc.vector, 1, 2, 4)
-        store(1, 2, 4)
+        silu(0, TILES)
+        for g in range(1, TILES):
+            add_skip(g)
+        apply_gate(0, 2)
+        apply_gate(2, TILES)
+        store(0, TILES)
+        for g in range(TILES, WINDOWS):
+            scale_skip(g)
+        for lo in range(TILES, WINDOWS, 2):
+            silu(lo, lo + 2)
+        for g in range(TILES, WINDOWS):
+            add_skip(g)
+        for lo in range(TILES, WINDOWS, 2):
+            apply_gate(lo, lo + 2)
+            store(lo, lo + 2)

from contextlib import ExitStack

import concourse.mybir as mybir

F32 = mybir.dt.float32
BF16 = mybir.dt.bfloat16
U32 = mybir.dt.uint32
U8 = mybir.dt.uint8
FP8X4 = mybir.dt.float8_e4m3fn_x4
ACT = mybir.ActivationFunctionType
ALU = mybir.AluOpType

P = 128
W = 128
R = 32
PACK = 4
TILES = 4
SETS = 2
WINDOWS = SETS * TILES
FLOPS = 2 * 2 * WINDOWS * W * W * W

K_COL = W
Q_COL = 2 * W
SHIFTS = (0, 2, 1, 3)
COPIED = 3


def tile_rows_win_ssd_skip_kernel(tc, kT, qT, dk, t, v, xs, ds, zg, out):
    nc = tc.nc
    with ExitStack() as ctx:
        sb = ctx.enter_context(tc.tile_pool(name="sb", bufs=1))
        ps = ctx.enter_context(tc.psum_pool(name="ps", bufs=1))
        ctx.enter_context(tc.manual_schedule())

        def tile(name, shape, dtype):
            return sb.tile(shape, dtype, name=name, align_bytes=64)

        def per_set(name, shape, dtype):
            return [tile(name + str(x), shape, dtype) for x in range(SETS)]

        k_raw = per_set("k_raw", [P, PACK, W], F32)
        q_raw = per_set("q_raw", [P, PACK, W], F32)
        v_raw = tile("v_raw", [P, SETS, PACK, W], F32)
        p_packed = per_set("p_packed", [P, PACK, W], BF16)
        k_bf = per_set("k_bf", [P, W, PACK], BF16)
        q_bf = per_set("q_bf", [P, W, PACK], BF16)
        v_bf = per_set("v_bf", [P, W, PACK], BF16)
        p_bf = per_set("p_bf", [P, W, PACK], BF16)
        p_codes = per_set("p_codes", [P, W], U32)
        p_scales = per_set("p_scales", [P, W], U8)
        v_codes = per_set("v_codes", [P, W], U32)
        v_scales = per_set("v_scales", [P, W], U8)
        kq_codes = tile("kq_codes", [P, 3 * W], U32)
        kq_scales = tile("kq_scales", [P, 3 * W], U8)
        k_scales_shifted = tile("k_scales_shifted", [P, 3 * W], U8)
        dk_packed = tile("dk_packed", [P, PACK, W], F32)
        t_packed = tile("t_packed", [P, 8], F32)
        dk_t = tile("dk_t", [P, PACK, W], F32)
        z_copied = tile("z_copied", [P, PACK, W], F32)
        k_codes = tile("k_codes", [P, W], U32)
        k_scales = tile("k_scales", [P, W], U8)
        q_codes = tile("q_codes", [P, W], U32)
        q_scales = tile("q_scales", [P, W], U8)
        dk_rows = tile("dk_rows", [P, TILES, W], F32)
        p_rows = tile("p_rows", [P, TILES, W], BF16)
        xs_sb = tile("xs_sb", [P, WINDOWS, W], F32)
        zg_sb = tile("zg_sb", [P, WINDOWS, W], F32)
        skip = tile("skip", [P, WINDOWS, W], F32)
        gate = tile("gate", [P, WINDOWS, W], F32)
        summed = tile("summed", [P, WINDOWS, W], F32)
        result = tile("result", [P, WINDOWS, W], F32)
        t_blocks = tile("t_blocks", [P, R], F32)
        t_cols = tile("t_cols", [P, R], F32)
        ds_blocks = tile("ds_blocks", [P, R], F32)
        ds_cols = tile("ds_cols", [P, R], F32)
        wide_banks = [ps.tile([P, PACK, W], F32, name="wide%d" % r) for r in range(TILES)]
        narrow_banks = [ps.tile([P, W], F32, name="narrow%d" % r) for r in range(TILES)]
        y_psum = [bank[:, 0, :] for bank in wide_banks] + [bank[:] for bank in narrow_banks]

        def rows(r):
            return slice(R * r, R * (r + 1))

        def load_packed(dst, src, x):
            windows = src[TILES * x : TILES * (x + 1)]
            nc.sync.dma_start(out=dst[:], in_=windows.rearrange("g (s j) c -> (g s) j c", j=PACK))

        def load_rows(dst, windows):
            nc.sync.dma_start(out=dst, in_=windows.rearrange("g a b -> a g b"))

        def load_blocks(queue, dst, windows):
            count = windows.shape[0]
            for a in range(TILES):
                queue.dma_start(
                    out=dst[R * a : R * a + count, :], in_=windows[:, rows(a), :].rearrange("g c o -> g (c o)")
                )

        def interleave(copy, dst, src):
            copy(out=dst[:], in_=src.rearrange("p j c -> p c j"))

        def quantize(codes, scales, src):
            nc.vector.quantize_mx(out=codes.bitcast(FP8X4), scales=scales, in_=src[:].rearrange("p c j -> p (c j)"))

        def product(dst, r, lhs_codes, lhs_scales, rhs_codes, rhs_scales):
            nc.tensor.matmul_mx(
                out=dst,
                lhsT=lhs_codes[rows(r)].bitcast(FP8X4),
                lhsT_scale=lhs_scales[rows(r)],
                rhs=rhs_codes[rows(r)].bitcast(FP8X4),
                rhs_scale=rhs_scales[rows(r)],
                start=True,
                stop=True,
            )

        def shifted_scores(r, shift):
            j = (r + shift) % PACK
            first = K_COL + R * (j - r)
            if shift % 2 == 0:
                scales = kq_scales[:, first : first + W]
            else:
                scales = k_scales_shifted[:, first - R : first - R + W]
            queries = slice(Q_COL, Q_COL + W)
            product(
                wide_banks[r][:, j, :],
                r,
                kq_codes[:, first : first + W],
                scales,
                kq_codes[:, queries],
                kq_scales[:, queries],
            )

        def values(x):
            quantize(p_codes[x][:], p_scales[x][:], p_bf[x])
            for r in range(TILES):
                product(y_psum[TILES * x + r], r, p_codes[x], p_scales[x], v_codes[x], v_scales[x])

        def scale_skip(g):
            nc.scalar.activation(out=skip[:, g, :], in_=xs_sb[:, g, :], func=ACT.Copy, scale=ds_cols[:, g : g + 1])

        def add_skip(g):
            nc.vector.tensor_tensor(out=summed[:, g, :], in0=y_psum[g], in1=skip[:, g, :], op=ALU.add)

        def silu(lo, hi):
            nc.scalar.activation(out=gate[:, lo:hi, :], in_=zg_sb[:, lo:hi, :], func=ACT.Silu)

        def apply_gate(lo, hi):
            nc.vector.tensor_tensor(
                out=result[:, lo:hi, :], in0=summed[:, lo:hi, :], in1=gate[:, lo:hi, :], op=ALU.mult
            )

        def store(lo, hi):
            nc.sync.dma_start(out=out[lo:hi].rearrange("g q e -> q g e"), in_=result[:, lo:hi, :])

        nc.scalar.dma_start(out=t_packed[:, 0:PACK], in_=t[0:TILES].rearrange("g (s j) o -> (g s) (j o)", j=PACK))

        nc.vector.memset(ds_cols[:], 0.0)
        nc.vector.memset(kq_codes[:, 0:K_COL], 0)
        nc.vector.memset(kq_scales[:].bitcast(U32), 0)
        nc.vector.memset(k_scales_shifted[:].bitcast(U32), 0)
        nc.gpsimd.memset(ds_blocks[:], 0.0)
        nc.scalar.activation(out=t_blocks[:], in_=ds_cols[:], func=ACT.Silu)

        for x in range(SETS):
            load_packed(k_raw[x], kT, x)
            load_packed(q_raw[x], qT, x)
        load_blocks(nc.sync, t_blocks, t[TILES:WINDOWS])
        load_blocks(nc.gpsimd, ds_blocks, ds)
        load_packed(dk_packed, dk, 0)
        load_rows(dk_rows[:], dk[TILES:WINDOWS])
        nc.sync.dma_start(out=v_raw[:], in_=v.rearrange("(x g) (s j) c -> (g s) x j c", x=SETS, j=PACK))
        load_rows(xs_sb[:, 0:TILES, :], xs[0:TILES])
        load_rows(zg_sb[:, 0:TILES, :], zg[0:TILES])

        nc.vector.tensor_copy(
            out=k_bf[0][:].rearrange("p (j s) u -> p j s u", j=PACK),
            in_=k_raw[0][:].rearrange("p u (s j) -> p j s u", j=PACK),
        )
        interleave(nc.vector.tensor_copy, q_bf[0], q_raw[0][:])
        quantize(kq_codes[:, K_COL : K_COL + W], kq_scales[:, K_COL : K_COL + W], k_bf[0])
        quantize(kq_codes[:, Q_COL : Q_COL + W], kq_scales[:, Q_COL : Q_COL + W], q_bf[0])
        nc.vector.tensor_copy(out=k_scales_shifted[:, K_COL - R : K_COL - R + W], in_=kq_scales[:, K_COL : K_COL + W])
        for shift in SHIFTS:
            shifted_scores(0, shift)
            shifted_scores(1, shift)

        interleave(nc.scalar.copy, k_bf[1], k_raw[1][:])
        interleave(nc.vector.tensor_copy, q_bf[1], q_raw[1][:])
        quantize(k_codes[:], k_scales[:], k_bf[1])
        quantize(q_codes[:], q_scales[:], q_bf[1])
        nc.vector.transpose(out=t_cols[:], in_=t_blocks[:])
        for r, shift in enumerate(SHIFTS):
            shifted_scores(2, shift)
            product(narrow_banks[r][:], r, k_codes, k_scales, q_codes, q_scales)
        for shift in SHIFTS:
            shifted_scores(3, shift)

        for j in range(PACK):
            nc.vector.tensor_scalar(
                out=dk_t[:, j, :], in0=dk_packed[:, j, :], scalar1=t_packed[:, j : j + 1], scalar2=None, op0=ALU.mult
            )
        for r in range(TILES):
            nc.vector.scalar_tensor_tensor(
                out=p_rows[:, r, :],
                in0=narrow_banks[r][:],
                scalar=t_cols[:, r : r + 1],
                in1=dk_rows[:, r, :],
                op0=ALU.mult,
                op1=ALU.mult,
            )
            nc.sync.dma_start(out=p_packed[1][rows(r)], in_=p_rows[:, r, :])
        load_rows(xs_sb[:, TILES:WINDOWS, :], xs[TILES:WINDOWS])
        load_rows(zg_sb[:, TILES:WINDOWS, :], zg[TILES:WINDOWS])

        for r in range(COPIED):
            nc.scalar.copy(out=z_copied[rows(r)], in_=wide_banks[r][rows(r)])
        last = rows(COPIED)
        nc.vector.tensor_tensor(out=p_packed[0][last], in0=wide_banks[COPIED][last], in1=dk_t[last], op=ALU.mult)
        copied = slice(0, R * COPIED)
        nc.vector.tensor_tensor(out=p_packed[0][copied], in0=z_copied[copied], in1=dk_t[copied], op=ALU.mult)

        nc.vector.transpose(out=ds_cols[:], in_=ds_blocks[:])
        for x in range(SETS):
            interleave(nc.scalar.copy, v_bf[x], v_raw[:, x])
        interleave(nc.vector.tensor_copy, p_bf[0], p_packed[0][:])
        quantize(v_codes[0][:], v_scales[0][:], v_bf[0])
        values(0)
        quantize(v_codes[1][:], v_scales[1][:], v_bf[1])
        for g in range(TILES):
            scale_skip(g)
        interleave(nc.vector.tensor_copy, p_bf[1], p_packed[1][:])
        add_skip(0)
        values(1)
        silu(0, TILES)
        for g in range(1, TILES):
            add_skip(g)
        apply_gate(0, 2)
        apply_gate(2, TILES)
        store(0, TILES)
        for g in range(TILES, WINDOWS):
            scale_skip(g)
        for lo in range(TILES, WINDOWS, 2):
            silu(lo, lo + 2)
        for g in range(TILES, WINDOWS):
            add_skip(g)
        for lo in range(TILES, WINDOWS, 2):
            apply_gate(lo, lo + 2)
            store(lo, lo + 2)
